import numpy as np
import ml_dtypes


def mxq(x, axis, fmt="e4m3"):
    dtype, down = {"e4m3": (ml_dtypes.float8_e4m3fn, 7), "e5m2": (ml_dtypes.float8_e5m2, 14)}[fmt]
    v = np.moveaxis(np.asarray(x, np.float32).astype(ml_dtypes.bfloat16).astype(np.float64), axis, -1)
    blocks = v.reshape(v.shape[:-1] + (-1, 32))
    amax = np.abs(blocks).max(-1, keepdims=True)
    byte = np.maximum(np.where(amax > 0, np.frexp(amax)[1] - 1 + 127, 0) - down, 1)
    scale = np.exp2(byte - 127.0)
    codes = (blocks / scale).astype(np.float32).astype(dtype).astype(np.float64)
    return np.moveaxis((codes * scale).reshape(v.shape), -1, axis)


WIDE = False


def mx_kscale(k):
    if not WIDE:
        return np.ones(k)
    levels = np.array([10, -10, 5, -5, 0])
    if k % 512:
        return np.exp2(np.random.permutation(np.resize(levels, k // 32))).repeat(32)
    a = np.empty((k // 512, 16))
    for p in range(k // 512):
        a[p, :8] = np.random.permutation(np.resize(levels, 8))
        for g in range(8):
            far = levels[np.abs(levels - a[p, g]) >= 10]
            a[p, g + 8] = far[np.random.randint(len(far))]
    return np.exp2(a.ravel()).repeat(32)


def f64(x):
    return np.asarray(x).astype(np.float64)


def striped(idx):
    return np.tile(idx.reshape(-1, 16).T, (8, 1)).astype(np.uint16)


def unstriped(offs):
    return offs[:16].T.reshape(-1).astype(np.int64)


def striped8(idx):
    return np.concatenate([x.reshape(-1, 16).T for x in idx]).astype(np.uint16)


def runs(offs, k):
    lists = np.stack([offs[16 * r : 16 * r + 16].T.reshape(-1) for r in range(8)]).astype(np.int64)
    return lists[np.arange(k) % 512 // 64]


def pack_weight(w):
    k, n = w.shape
    w = f64(np.asarray(w, np.float32).astype(ml_dtypes.bfloat16)).reshape(k // 32, 32, n)
    amax = np.abs(w).max(1)
    byte = np.clip(np.where(amax > 0, np.frexp(amax)[1] - 1 + 127 - 7, 1), 1, 254)
    scaled = (w * np.exp2(127.0 - byte)[:, None, :]).reshape(k, n).astype(np.float32)
    words = np.ascontiguousarray(scaled.reshape(k // 512, 128, 4, n).transpose(0, 1, 3, 2)).astype(ml_dtypes.float8_e4m3fn).view(np.uint8)
    return words, np.ascontiguousarray(byte.astype(np.uint8).reshape(k // 512, 16, n))


def unpack_weight(words, scales):
    g, p, n, _ = words.shape
    vals = np.ascontiguousarray(words).view(ml_dtypes.float8_e4m3fn).astype(np.float64) * np.repeat(np.exp2(scales.astype(np.float64) - 127.0), 8, axis=1)[..., None]
    return vals.transpose(0, 1, 3, 2).reshape(g * 512, n)


K, T, S, N, H = 512, 2048, 256, 512, 512


def setup_inputs():
    n = np.random.standard_normal
    s = mx_kscale(K)[:, None]
    u = mx_kscale(H)
    packed_xT = pack_weight(n((K, T)) * s)
    return {
        "x_words": packed_xT[0],
        "x_scales": packed_xT[1],
        "w1": (n((K, H)) / np.sqrt(K) / s).astype(np.float32),
        "w2": (n((K, H)) / np.sqrt(K) / s).astype(np.float32),
        "gn": (np.random.uniform(0.5, 1.5, (H, 1)) * u[:, None]).astype(np.float32),
        "w3": (n((H, N)) / np.sqrt(H) / u[:, None]).astype(np.float32),
        "offs": striped(np.random.permutation(T)[:S]),
        "two": striped(np.random.permutation(T)[:S]),
        "n1": striped8(np.stack([np.random.permutation(S) for _ in range(8)])),
        "n2": striped8(np.stack([np.random.permutation(S) for _ in range(8)])),
        "n3": striped(np.random.permutation(S)),
    }


def reference(x_words, x_scales, w1, w2, gn, w3, offs, two, n1, n2, n3):
    xq = unpack_weight(x_words, x_scales)[:, unstriped(offs)]
    y = mxq(f64(w1), 0, "e4m3").T @ xq
    x_two = unpack_weight(x_words, x_scales)[:, unstriped(two)]
    d = mxq(f64(w2), 0, "e4m3").T @ x_two
    z = f64(gn) * ((y - (y[np.arange(H)[:, None], runs(n1, H)])) / (np.abs(d) + np.abs(d[np.arange(H)[:, None], runs(n2, H)]) + 0.5))
    h = mxq(f64(w3), 0, "e4m3").T @ mxq(z, 0, "e4m3")
    st = h - h[:, unstriped(n3)]
    return st - (0.5 * st[:, unstriped(n3)])

@@ -1,0 +1,208 @@
+from contextlib import ExitStack
+
+import concourse.mybir as mybir
+
+K, T, S, H, N = 512, 2048, 256, 512, 512
+FLOPS = 2 * K * H * S * 2 + 2 * H * N * S
+
+F32 = mybir.dt.float32
+BF16 = mybir.dt.bfloat16
+I32 = mybir.dt.int32
+U32 = mybir.dt.uint32
+U16 = mybir.dt.uint16
+U8 = mybir.dt.uint8
+FP8X4 = mybir.dt.float8_e4m3fn_x4
+ALU = mybir.AluOpType
+ACT = mybir.ActivationFunctionType
+
+P = 128
+PACK = 4
+HALF = S // 2
+LIST_COLS = S // 16
+SPARE = 8
+
+
+def tile_picked_twlnormbtwice_none_p_kernel(tc, x_words, x_scales, w1, w2, gn, w3, offs, two, n1, n2, n3, out):
+    nc = tc.nc
+    with ExitStack() as ctx:
+        lists = ctx.enter_context(tc.tile_pool(name="lists", bufs=1))
+        keep = ctx.enter_context(tc.tile_pool(name="keep", bufs=1))
+        psum = ctx.enter_context(tc.psum_pool(name="psum", bufs=1))
+
+        offs_sb = lists.tile([P, LIST_COLS], U16, name="offs_sb")
+        two_sb = lists.tile([P, LIST_COLS], U16, name="two_sb")
+        n1_sb = lists.tile([P, LIST_COLS], U16, name="n1_sb")
+        n2_sb = lists.tile([P, LIST_COLS], U16, name="n2_sb")
+        n3_sb = lists.tile([P, LIST_COLS], U16, name="n3_sb")
+
+        x_table = keep.tile([P, T], U32, name="x_table")
+        scale_table = keep.tile([P, T], U8, name="scale_table")
+        w1_raw = keep.tile([P, PACK, H], F32, name="w1_raw")
+        w2_raw = keep.tile([P, PACK, H], F32, name="w2_raw")
+        w3_raw = keep.tile([P, PACK, N], F32, name="w3_raw")
+        gain = keep.tile([P, PACK], F32, name="gain")
+        h_rows = [keep.tile([P, S + SPARE], F32, name=f"h_rows{t}") for t in range(PACK)]
+        st_rows = [keep.tile([P, S + SPARE], F32, name=f"st_rows{t}") for t in range(PACK)]
+
+        nc.gpsimd.memset(scale_table[:].bitcast(I32), 0)
+        for list_sb, list_in in ((two_sb, two), (offs_sb, offs), (n2_sb, n2), (n1_sb, n1), (n3_sb, n3)):
+            nc.sync.dma_start(list_sb[:], list_in)
+        nc.sync.dma_start(out=w2_raw[:], in_=w2.rearrange("(p j) c -> p j c", j=PACK))
+        for q in range(4):
+            nc.scalar.dma_start(
+                out=scale_table[32 * q : 32 * q + 4, :].bitcast(I32),
+                in_=x_scales[0, 4 * q : 4 * q + 4, :].bitcast(I32),
+            )
+        nc.sync.dma_start(
+            out=x_table[:].bitcast(I32), in_=x_words[0].rearrange("p n t -> p (n t)").bitcast(I32)
+        )
+        nc.sync.dma_start(out=w1_raw[:], in_=w1.rearrange("(p j) c -> p j c", j=PACK))
+        nc.sync.dma_start(out=w3_raw[:], in_=w3.rearrange("(p j) c -> p j c", j=PACK))
+        nc.gpsimd.dma_start(out=gain[:], in_=gn.rearrange("(p t) o -> p (t o)", t=PACK))
+        for rows in h_rows + st_rows:
+            nc.gpsimd.memset(rows[:, S:], 0.0)
+
+        def mx_tiles(name, width):
+            codes = keep.tile([P, width], U32, name=name + "_codes", align_bytes=64)
+            scales = keep.tile([P, width], U8, name=name + "_scales", align_bytes=64)
+            return codes, scales
+
+        def quantise(codes, scales, rounded, first, width):
+            nc.vector.quantize_mx(
+                out=codes[:, first : first + width].bitcast(FP8X4),
+                scales=scales[:, first : first + width],
+                in_=rounded[:, PACK * first : PACK * (first + width)],
+            )
+
+        def product(acc, w_mx, t, moving_mx):
+            cols = slice(P * t, P * (t + 1))
+            nc.tensor.matmul_mx(
+                out=acc,
+                lhsT=w_mx[0][:, cols].bitcast(FP8X4),
+                lhsT_scale=w_mx[1][:, cols],
+                rhs=moving_mx[0][:].bitcast(FP8X4),
+                rhs_scale=moving_mx[1][:],
+                start=True,
+                stop=True,
+            )
+
+        def dealt_views(rounded, raw):
+            return (
+                rounded[:].rearrange("p (t m j) -> p m j t", t=PACK, j=PACK),
+                raw[:].rearrange("p j (m t) -> p m j t", t=PACK),
+            )
+
+        w2_rounded = keep.tile([P, PACK * H], BF16, name="w2_rounded", align_bytes=64)
+        dst, src = dealt_views(w2_rounded, w2_raw)
+        nc.vector.tensor_copy(out=dst[:, :80], in_=src[:, :80])
+        nc.scalar.copy(out=dst[:, 80:], in_=src[:, 80:])
+        w2_mx = mx_tiles("w2", H)
+        quantise(*w2_mx, w2_rounded, 0, H)
+
+        two_mx = mx_tiles("x_two", S)
+        offs_mx = mx_tiles("x_offs", S)
+        nc.vector.tensor_copy(two_mx[1][:], scale_table[:].indirect(two_sb[:]))
+        nc.vector.tensor_copy(offs_mx[1][:], scale_table[:].indirect(offs_sb[:]))
+        nc.vector.tensor_copy(two_mx[0][:], x_table[:].indirect(two_sb[:]))
+        nc.vector.tensor_copy(offs_mx[0][:], x_table[:].indirect(offs_sb[:]))
+
+        def half_list(list_sb, half):
+            return list_sb[:, half * LIST_COLS // 2 : (half + 1) * LIST_COLS // 2]
+
+        d_fetched = keep.tile([P, PACK, S], F32, name="d_fetched")
+        denom = keep.tile([P, PACK, S], F32, name="denom")
+        root = keep.tile([P, PACK, S], F32, name="root")
+        factor = keep.tile([P, PACK, S], F32, name="factor")
+        d_abs = [keep.tile([P, S], F32, name=f"d_abs{t}") for t in range(PACK)]
+        for t in range(PACK):
+            d_acc = psum.tile([P, S], F32, name=f"d_acc{t}", tag=f"bank{t}")
+            product(d_acc[:], w2_mx, t, two_mx)
+            nc.scalar.activation(d_abs[t][:], d_acc[:], ACT.Abs)
+            for half in range(2):
+                nc.scalar.activation(
+                    d_fetched[:, t, half * HALF : (half + 1) * HALF],
+                    d_abs[t][:].indirect(half_list(n2_sb, half)),
+                    ACT.Copy,
+                )
+
+        w1_rounded = keep.tile([P, PACK * H], BF16, name="w1_rounded", align_bytes=64)
+        dst, src = dealt_views(w1_rounded, w1_raw)
+        nc.vector.tensor_copy(out=dst, in_=src)
+        for t in range(PACK):
+            nc.vector.scalar_tensor_tensor(
+                out=denom[:, t, :], in0=d_abs[t][:], scalar=0.5, in1=d_fetched[:, t, :], op0=ALU.add, op1=ALU.add
+            )
+        w1_mx = mx_tiles("w1", H)
+        quantise(*w1_mx, w1_rounded, 0, H)
+
+        y_acc = [psum.tile([P, 2, S], F32, name=f"y_acc{b}", tag=f"y_bank{b}") for b in range(2)]
+        y_rows = [keep.tile([P, S], F32, name=f"y_rows{t}") for t in range(PACK)]
+        for b in range(2):
+            for e in range(2):
+                product(y_acc[b][:, e, :], w1_mx, 2 * b + e, offs_mx)
+            for e in range(2):
+                nc.vector.tensor_copy(out=y_rows[2 * b + e][:], in_=y_acc[b][:, e, :])
+
+        for b in range(2):
+            nc.scalar.activation(root[:, 2 * b : 2 * b + 2, :], denom[:, 2 * b : 2 * b + 2, :], ACT.Abs_reciprocal_sqrt)
+        for t in range(PACK):
+            nc.vector.scalar_tensor_tensor(
+                out=factor[:, t, :], in0=root[:, t, :], scalar=gain[:, t : t + 1], in1=root[:, t, :],
+                op0=ALU.mult, op1=ALU.mult,
+            )
+
+        w3_rounded = keep.tile([P, PACK * N], BF16, name="w3_rounded", align_bytes=64)
+        w3_mx = mx_tiles("w3", N)
+
+        def round_w3(t):
+            nc.vector.tensor_copy(
+                out=w3_rounded[:, PACK * P * t : PACK * P * (t + 1)].rearrange("p (c i j) -> p c j i", i=4, j=PACK),
+                in_=w3_raw[:, :, P * t : P * (t + 1)].rearrange("p j (c i) -> p c j i", i=4),
+            )
+
+        round_w3(0)
+
+        z_rounded = keep.tile([P, PACK * S], BF16, name="z_rounded", align_bytes=64)
+        z_mx = mx_tiles("z", S)
+        for half in range(2):
+            cols = slice(half * HALF, (half + 1) * HALF)
+            y_fetched = keep.tile([P, PACK, HALF], F32, name=f"y_fetched{half}")
+            diff = keep.tile([P, PACK, HALF], F32, name=f"diff{half}")
+            for t in range(PACK):
+                nc.scalar.activation(y_fetched[:, t, :], y_rows[t][:].indirect(half_list(n1_sb, half)), ACT.Copy)
+            for b in range(2):
+                nc.vector.tensor_tensor(
+                    out=diff[:, 2 * b : 2 * b + 2, :], in0=y_acc[b][:, :, cols],
+                    in1=y_fetched[:, 2 * b : 2 * b + 2, :], op=ALU.subtract,
+                )
+            if half == 0:
+                quantise(*w3_mx, w3_rounded, 0, P)
+            nc.vector.tensor_tensor(
+                out=z_rounded[:, half * PACK * HALF : (half + 1) * PACK * HALF].rearrange(
+                    "p (c i t) -> p c t i", i=4, t=PACK
+                ),
+                in0=diff[:].rearrange("p t (c i) -> p c t i", i=4),
+                in1=factor[:, :, cols].rearrange("p t (c i) -> p c t i", i=4),
+                op=ALU.mult,
+            )
+        for half in range(2):
+            quantise(*z_mx, z_rounded, half * HALF, HALF)
+
+        for t in range(PACK):
+            h_acc = psum.tile([P, S], F32, name=f"h_acc{t}", tag=f"bank{t}")
+            product(h_acc[:], w3_mx, t, z_mx)
+            if t + 1 < PACK:
+                round_w3(t + 1)
+            nc.vector.tensor_copy(out=h_rows[t][:, :S], in_=h_acc[:])
+            if t + 1 < PACK:
+                quantise(*w3_mx, w3_rounded, P * (t + 1), P)
+            h_fetched = keep.tile([P, S], F32, name=f"h_fetched{t}")
+            nc.scalar.activation(h_fetched[:], h_rows[t][:].indirect(n3_sb[:]), ACT.Copy)
+            nc.vector.tensor_tensor(out=st_rows[t][:, :S], in0=h_acc[:], in1=h_fetched[:], op=ALU.subtract)
+            st_fetched = keep.tile([P, S], F32, name=f"st_fetched{t}")
+            nc.scalar.activation(st_fetched[:], st_rows[t][:].indirect(n3_sb[:]), ACT.Copy)
+            result = keep.tile([P, S], F32, name=f"result{t}")
+            nc.vector.scalar_tensor_tensor(
+                out=result[:], in0=st_fetched[:], scalar=-0.5, in1=st_rows[t][:, :S], op0=ALU.mult, op1=ALU.add
+            )
+            nc.sync.dma_start(out=out[P * t : P * (t + 1), :], in_=result[:])

@@ -37,30 +37,38 @@ def tile_picked_twlnormbtwice_none_p_kernel(tc, x_words, x_scales, w1, w2, gn, w
 
         x_table = keep.tile([P, T], U32, name="x_table")
         scale_table = keep.tile([P, T], U8, name="scale_table")
-        w1_raw = keep.tile([P, PACK, H], F32, name="w1_raw")
+        w1_raw = [keep.tile([P, PACK, H // 2], F32, name=f"w1_raw{half}") for half in range(2)]
         w2_raw = keep.tile([P, PACK, H], F32, name="w2_raw")
         w3_raw = keep.tile([P, PACK, N], F32, name="w3_raw")
         gain = keep.tile([P, PACK], F32, name="gain")
         h_rows = [keep.tile([P, S + SPARE], F32, name=f"h_rows{t}") for t in range(PACK)]
         st_rows = [keep.tile([P, S + SPARE], F32, name=f"st_rows{t}") for t in range(PACK)]
 
-        nc.gpsimd.memset(scale_table[:].bitcast(I32), 0)
-        for list_sb, list_in in ((two_sb, two), (offs_sb, offs), (n2_sb, n2), (n1_sb, n1), (n3_sb, n3)):
+        nc.vector.memset(scale_table[:].bitcast(I32), 0)
+        for list_sb, list_in in ((two_sb, two), (offs_sb, offs), (n2_sb, n2)):
             nc.sync.dma_start(list_sb[:], list_in)
         nc.sync.dma_start(out=w2_raw[:], in_=w2.rearrange("(p j) c -> p j c", j=PACK))
         for q in range(4):
-            nc.scalar.dma_start(
+            nc.sync.dma_start(
                 out=scale_table[32 * q : 32 * q + 4, :].bitcast(I32),
                 in_=x_scales[0, 4 * q : 4 * q + 4, :].bitcast(I32),
             )
         nc.sync.dma_start(
             out=x_table[:].bitcast(I32), in_=x_words[0].rearrange("p n t -> p (n t)").bitcast(I32)
         )
-        nc.sync.dma_start(out=w1_raw[:], in_=w1.rearrange("(p j) c -> p j c", j=PACK))
+        for half in range(2):
+            nc.sync.dma_start(
+                out=w1_raw[half][:],
+                in_=w1[:, half * H // 2 : (half + 1) * H // 2].rearrange("(p j) c -> p j c", j=PACK),
+            )
+        nc.sync.dma_start(n1_sb[:], n1)
         nc.sync.dma_start(out=w3_raw[:], in_=w3.rearrange("(p j) c -> p j c", j=PACK))
-        nc.gpsimd.dma_start(out=gain[:], in_=gn.rearrange("(p t) o -> p (t o)", t=PACK))
+        nc.sync.dma_start(n3_sb[:], n3)
+        nc.sync.dma_start(out=gain[:], in_=gn.rearrange("(p t) o -> p (t o)", t=PACK))
         for rows in h_rows + st_rows:
-            nc.gpsimd.memset(rows[:, S:], 0.0)
+            nc.vector.memset(rows[:, S:], 0.0)
+        warm = keep.tile([P, SPARE], F32, name="warm")
+        nc.scalar.activation(warm[:], h_rows[0][:, S:], ACT.Abs_reciprocal_sqrt, bias=1.0)
 
         def mx_tiles(name, width):
             codes = keep.tile([P, width], U32, name=name + "_codes", align_bytes=64)
@@ -94,23 +102,21 @@ def tile_picked_twlnormbtwice_none_p_kernel(tc, x_words, x_scales, w1, w2, gn, w
 
         w2_rounded = keep.tile([P, PACK * H], BF16, name="w2_rounded", align_bytes=64)
         dst, src = dealt_views(w2_rounded, w2_raw)
-        nc.vector.tensor_copy(out=dst[:, :80], in_=src[:, :80])
-        nc.scalar.copy(out=dst[:, 80:], in_=src[:, 80:])
+        nc.vector.tensor_copy(out=dst[:, :44], in_=src[:, :44])
+        nc.scalar.copy(out=dst[:, 44:], in_=src[:, 44:])
         w2_mx = mx_tiles("w2", H)
-        quantise(*w2_mx, w2_rounded, 0, H)
-
         two_mx = mx_tiles("x_two", S)
         offs_mx = mx_tiles("x_offs", S)
         nc.vector.tensor_copy(two_mx[1][:], scale_table[:].indirect(two_sb[:]))
-        nc.vector.tensor_copy(offs_mx[1][:], scale_table[:].indirect(offs_sb[:]))
+        quantise(*w2_mx, w2_rounded, 0, H)
         nc.vector.tensor_copy(two_mx[0][:], x_table[:].indirect(two_sb[:]))
+        nc.vector.tensor_copy(offs_mx[1][:], scale_table[:].indirect(offs_sb[:]))
         nc.vector.tensor_copy(offs_mx[0][:], x_table[:].indirect(offs_sb[:]))
 
         def half_list(list_sb, half):
             return list_sb[:, half * LIST_COLS // 2 : (half + 1) * LIST_COLS // 2]
 
         d_fetched = keep.tile([P, PACK, S], F32, name="d_fetched")
-        denom = keep.tile([P, PACK, S], F32, name="denom")
         root = keep.tile([P, PACK, S], F32, name="root")
         factor = keep.tile([P, PACK, S], F32, name="factor")
         d_abs = [keep.tile([P, S], F32, name=f"d_abs{t}") for t in range(PACK)]
@@ -125,15 +131,31 @@ def tile_picked_twlnormbtwice_none_p_kernel(tc, x_words, x_scales, w1, w2, gn, w
                     ACT.Copy,
                 )
 
-        w1_rounded = keep.tile([P, PACK * H], BF16, name="w1_rounded", align_bytes=64)
-        dst, src = dealt_views(w1_rounded, w1_raw)
-        nc.vector.tensor_copy(out=dst, in_=src)
-        for t in range(PACK):
+        def denominator(t, denom):
             nc.vector.scalar_tensor_tensor(
-                out=denom[:, t, :], in0=d_abs[t][:], scalar=0.5, in1=d_fetched[:, t, :], op0=ALU.add, op1=ALU.add
+                out=denom, in0=d_abs[t][:], scalar=0.5, in1=d_fetched[:, t, :], op0=ALU.add, op1=ALU.add
+            )
+            nc.scalar.activation(root[:, t, :], denom, ACT.Abs_reciprocal_sqrt)
+
+        def gain_over_denominator(t):
+            nc.vector.scalar_tensor_tensor(
+                out=factor[:, t, :], in0=root[:, t, :], scalar=gain[:, t : t + 1], in1=root[:, t, :],
+                op0=ALU.mult, op1=ALU.mult,
+            )
+
+        w1_rounded = keep.tile([P, PACK * H], BF16, name="w1_rounded", align_bytes=64)
+        dst = w1_rounded[:].rearrange("p (t m j) -> p m j t", t=PACK, j=PACK)
+        for half in range(2):
+            nc.vector.tensor_copy(
+                out=dst[:, half * P // 2 : (half + 1) * P // 2],
+                in_=w1_raw[half][:].rearrange("p j (m t) -> p m j t", t=PACK),
             )
         w1_mx = mx_tiles("w1", H)
-        quantise(*w1_mx, w1_rounded, 0, H)
+        for b in range(2):
+            quantise(*w1_mx, w1_rounded, 2 * P * b, 2 * P)
+        denom_01 = keep.tile([P, 2, S], F32, name="denom_01", tag="w1_rounded", align_bytes=64)
+        for t in range(2):
+            denominator(t, denom_01[:, t, :])
 
         y_acc = [psum.tile([P, 2, S], F32, name=f"y_acc{b}", tag=f"y_bank{b}") for b in range(2)]
         y_rows = [keep.tile([P, S], F32, name=f"y_rows{t}") for t in range(PACK)]
@@ -142,41 +164,49 @@ def tile_picked_twlnormbtwice_none_p_kernel(tc, x_words, x_scales, w1, w2, gn, w
                 product(y_acc[b][:, e, :], w1_mx, 2 * b + e, offs_mx)
             for e in range(2):
                 nc.vector.tensor_copy(out=y_rows[2 * b + e][:], in_=y_acc[b][:, e, :])
-
-        for b in range(2):
-            nc.scalar.activation(root[:, 2 * b : 2 * b + 2, :], denom[:, 2 * b : 2 * b + 2, :], ACT.Abs_reciprocal_sqrt)
-        for t in range(PACK):
-            nc.vector.scalar_tensor_tensor(
-                out=factor[:, t, :], in0=root[:, t, :], scalar=gain[:, t : t + 1], in1=root[:, t, :],
-                op0=ALU.mult, op1=ALU.mult,
-            )
-
-        w3_rounded = keep.tile([P, PACK * N], BF16, name="w3_rounded", align_bytes=64)
+        denom_23 = keep.tile([P, 2, S], F32, name="denom_23", tag="w1_codes", align_bytes=64)
+        for t in range(2):
+            denominator(2 + t, denom_23[:, t, :])
+        y_fetched = keep.tile([P, 2, PACK, HALF], F32, name="y_fetched", tag="w1_codes", align_bytes=64)
+        for half in range(2):
+            for t in range(PACK):
+                nc.scalar.activation(
+                    y_fetched[:, half, t, :], y_rows[t][:].indirect(half_list(n1_sb, half)), ACT.Copy
+                )
         w3_mx = mx_tiles("w3", N)
+        w3_rounded = [keep.tile([P, PACK * P], BF16, name=f"w3_rounded{t}", align_bytes=64) for t in range(PACK)]
 
         def round_w3(t):
             nc.vector.tensor_copy(
-                out=w3_rounded[:, PACK * P * t : PACK * P * (t + 1)].rearrange("p (c i j) -> p c j i", i=4, j=PACK),
+                out=w3_rounded[t][:].rearrange("p (c i j) -> p c j i", i=4, j=PACK),
                 in_=w3_raw[:, :, P * t : P * (t + 1)].rearrange("p j (c i) -> p c j i", i=4),
             )
 
+        def quantise_w3(t):
+            cols = slice(P * t, P * (t + 1))
+            nc.vector.quantize_mx(out=w3_mx[0][:, cols].bitcast(FP8X4), scales=w3_mx[1][:, cols], in_=w3_rounded[t][:])
+
         round_w3(0)
+        gain_over_denominator(0)
+        gain_over_denominator(1)
+        quantise_w3(0)
+        gain_over_denominator(2)
+        round_w3(1)
+        gain_over_denominator(3)
+        quantise_w3(1)
 
         z_rounded = keep.tile([P, PACK * S], BF16, name="z_rounded", align_bytes=64)
         z_mx = mx_tiles("z", S)
         for half in range(2):
             cols = slice(half * HALF, (half + 1) * HALF)
-            y_fetched = keep.tile([P, PACK, HALF], F32, name=f"y_fetched{half}")
             diff = keep.tile([P, PACK, HALF], F32, name=f"diff{half}")
-            for t in range(PACK):
-                nc.scalar.activation(y_fetched[:, t, :], y_rows[t][:].indirect(half_list(n1_sb, half)), ACT.Copy)
             for b in range(2):
                 nc.vector.tensor_tensor(
                     out=diff[:, 2 * b : 2 * b + 2, :], in0=y_acc[b][:, :, cols],
-                    in1=y_fetched[:, 2 * b : 2 * b + 2, :], op=ALU.subtract,
+                    in1=y_fetched[:, half, 2 * b : 2 * b + 2, :], op=ALU.subtract,
                 )
-            if half == 0:
-                quantise(*w3_mx, w3_rounded, 0, P)
+                if half == 1 and b == 0:
+                    quantise(*z_mx, z_rounded, 0, HALF)
             nc.vector.tensor_tensor(
                 out=z_rounded[:, half * PACK * HALF : (half + 1) * PACK * HALF].rearrange(
                     "p (c i t) -> p c t i", i=4, t=PACK
@@ -185,24 +215,41 @@ def tile_picked_twlnormbtwice_none_p_kernel(tc, x_words, x_scales, w1, w2, gn, w
                 in1=factor[:, :, cols].rearrange("p t (c i) -> p c t i", i=4),
                 op=ALU.mult,
             )
-        for half in range(2):
-            quantise(*z_mx, z_rounded, half * HALF, HALF)
+        round_w3(2)
+        quantise(*z_mx, z_rounded, HALF, HALF)
+        quantise_w3(2)
 
-        for t in range(PACK):
-            h_acc = psum.tile([P, S], F32, name=f"h_acc{t}", tag=f"bank{t}")
-            product(h_acc[:], w3_mx, t, z_mx)
-            if t + 1 < PACK:
-                round_w3(t + 1)
-            nc.vector.tensor_copy(out=h_rows[t][:, :S], in_=h_acc[:])
-            if t + 1 < PACK:
-                quantise(*w3_mx, w3_rounded, P * (t + 1), P)
-            h_fetched = keep.tile([P, S], F32, name=f"h_fetched{t}")
-            nc.scalar.activation(h_fetched[:], h_rows[t][:].indirect(n3_sb[:]), ACT.Copy)
-            nc.vector.tensor_tensor(out=st_rows[t][:, :S], in0=h_acc[:], in1=h_fetched[:], op=ALU.subtract)
-            st_fetched = keep.tile([P, S], F32, name=f"st_fetched{t}")
-            nc.scalar.activation(st_fetched[:], st_rows[t][:].indirect(n3_sb[:]), ACT.Copy)
+        h_acc = [psum.tile([P, S], F32, name=f"h_acc{t}", tag=f"bank{t}") for t in range(PACK)]
+        h_fetched = [keep.tile([P, S], F32, name=f"h_fetched{t}") for t in range(PACK)]
+        st_fetched = [keep.tile([P, S], F32, name=f"st_fetched{t}") for t in range(PACK)]
+
+        def make_h(t):
+            product(h_acc[t][:], w3_mx, t, z_mx)
+            nc.vector.tensor_copy(out=h_rows[t][:, :S], in_=h_acc[t][:])
+            nc.scalar.activation(h_fetched[t][:], h_rows[t][:].indirect(n3_sb[:]), ACT.Copy)
+
+        def make_st(t):
+            nc.vector.tensor_tensor(out=st_rows[t][:, :S], in0=h_acc[t][:], in1=h_fetched[t][:], op=ALU.subtract)
+            nc.scalar.activation(st_fetched[t][:], st_rows[t][:].indirect(n3_sb[:]), ACT.Copy)
+
+        def make_out(t):
             result = keep.tile([P, S], F32, name=f"result{t}")
             nc.vector.scalar_tensor_tensor(
-                out=result[:], in0=st_fetched[:], scalar=-0.5, in1=st_rows[t][:, :S], op0=ALU.mult, op1=ALU.add
+                out=result[:], in0=st_fetched[t][:], scalar=-0.5, in1=st_rows[t][:, :S], op0=ALU.mult, op1=ALU.add
             )
             nc.sync.dma_start(out=out[P * t : P * (t + 1), :], in_=result[:])
+
+        make_h(0)
+        make_h(1)
+        round_w3(3)
+        make_st(0)
+        quantise_w3(3)
+        make_h(2)
+        make_st(1)
+        make_h(3)
+        make_out(0)
+        make_st(2)
+        make_out(1)
+        make_st(3)
+        make_out(2)
+        make_out(3)

@@ -20,6 +20,7 @@ PACK = 4
 HALF = S // 2
 LIST_COLS = S // 16
 SPARE = 8
+PIECES = ((0, 128), (128, 128))
 
 
 def tile_picked_twlnormbtwice_none_p_kernel(tc, x_words, x_scales, w1, w2, gn, w3, offs, two, n1, n2, n3, out):
@@ -48,10 +49,10 @@ def tile_picked_twlnormbtwice_none_p_kernel(tc, x_words, x_scales, w1, w2, gn, w
         for list_sb, list_in in ((two_sb, two), (offs_sb, offs), (n2_sb, n2)):
             nc.sync.dma_start(list_sb[:], list_in)
         nc.sync.dma_start(out=w2_raw[:], in_=w2.rearrange("(p j) c -> p j c", j=PACK))
-        for q in range(4):
+        for r in range(4):
             nc.sync.dma_start(
-                out=scale_table[32 * q : 32 * q + 4, :].bitcast(I32),
-                in_=x_scales[0, 4 * q : 4 * q + 4, :].bitcast(I32),
+                out=scale_table[r:P:32, :].bitcast(I32),
+                in_=x_scales[0, r:16:4, :].bitcast(I32),
             )
         nc.sync.dma_start(
             out=x_table[:].bitcast(I32), in_=x_words[0].rearrange("p n t -> p (n t)").bitcast(I32)
@@ -88,28 +89,28 @@ def tile_picked_twlnormbtwice_none_p_kernel(tc, x_words, x_scales, w1, w2, gn, w
                 out=acc,
                 lhsT=w_mx[0][:, cols].bitcast(FP8X4),
                 lhsT_scale=w_mx[1][:, cols],
-                rhs=moving_mx[0][:].bitcast(FP8X4),
-                rhs_scale=moving_mx[1][:],
+                rhs=moving_mx[0].bitcast(FP8X4),
+                rhs_scale=moving_mx[1],
                 start=True,
                 stop=True,
             )
 
         def dealt_views(rounded, raw):
             return (
-                rounded[:].rearrange("p (t m j) -> p m j t", t=PACK, j=PACK),
-                raw[:].rearrange("p j (m t) -> p m j t", t=PACK),
+                rounded[:].rearrange("p (t m i j) -> p m j i t", t=PACK, i=2, j=PACK),
+                raw[:].rearrange("p j (m i t) -> p m j i t", i=2, t=PACK),
             )
 
         w2_rounded = keep.tile([P, PACK * H], BF16, name="w2_rounded", align_bytes=64)
         dst, src = dealt_views(w2_rounded, w2_raw)
-        nc.vector.tensor_copy(out=dst[:, :44], in_=src[:, :44])
-        nc.scalar.copy(out=dst[:, 44:], in_=src[:, 44:])
+        nc.vector.tensor_copy(out=dst[:, :42], in_=src[:, :42])
+        nc.scalar.copy(out=dst[:, 42:], in_=src[:, 42:])
         w2_mx = mx_tiles("w2", H)
         two_mx = mx_tiles("x_two", S)
-        offs_mx = mx_tiles("x_offs", S)
         nc.vector.tensor_copy(two_mx[1][:], scale_table[:].indirect(two_sb[:]))
         quantise(*w2_mx, w2_rounded, 0, H)
         nc.vector.tensor_copy(two_mx[0][:], x_table[:].indirect(two_sb[:]))
+        offs_mx = mx_tiles("x_offs", S)
         nc.vector.tensor_copy(offs_mx[1][:], scale_table[:].indirect(offs_sb[:]))
         nc.vector.tensor_copy(offs_mx[0][:], x_table[:].indirect(offs_sb[:]))
 
@@ -122,7 +123,7 @@ def tile_picked_twlnormbtwice_none_p_kernel(tc, x_words, x_scales, w1, w2, gn, w
         d_abs = [keep.tile([P, S], F32, name=f"d_abs{t}") for t in range(PACK)]
         for t in range(PACK):
             d_acc = psum.tile([P, S], F32, name=f"d_acc{t}", tag=f"bank{t}")
-            product(d_acc[:], w2_mx, t, two_mx)
+            product(d_acc[:], w2_mx, t, (two_mx[0][:], two_mx[1][:]))
             nc.scalar.activation(d_abs[t][:], d_acc[:], ACT.Abs)
             for half in range(2):
                 nc.scalar.activation(
@@ -144,40 +145,45 @@ def tile_picked_twlnormbtwice_none_p_kernel(tc, x_words, x_scales, w1, w2, gn, w
             )
 
         w1_rounded = keep.tile([P, PACK * H], BF16, name="w1_rounded", align_bytes=64)
-        dst = w1_rounded[:].rearrange("p (t m j) -> p m j t", t=PACK, j=PACK)
+        dst = w1_rounded[:].rearrange("p (t m i j) -> p m j i t", t=PACK, i=2, j=PACK)
         for half in range(2):
             nc.vector.tensor_copy(
-                out=dst[:, half * P // 2 : (half + 1) * P // 2],
-                in_=w1_raw[half][:].rearrange("p j (m t) -> p m j t", t=PACK),
+                out=dst[:, half * P // 4 : (half + 1) * P // 4],
+                in_=w1_raw[half][:].rearrange("p j (m i t) -> p m j i t", i=2, t=PACK),
             )
         w1_mx = mx_tiles("w1", H)
         for b in range(2):
             quantise(*w1_mx, w1_rounded, 2 * P * b, 2 * P)
-        denom_01 = keep.tile([P, 2, S], F32, name="denom_01", tag="w1_rounded", align_bytes=64)
+        denom_01 = keep.tile([P, 2, S], F32, name="denom_01", tag="w1_raw1")
         for t in range(2):
             denominator(t, denom_01[:, t, :])
 
         y_acc = [psum.tile([P, 2, S], F32, name=f"y_acc{b}", tag=f"y_bank{b}") for b in range(2)]
-        y_rows = [keep.tile([P, S], F32, name=f"y_rows{t}") for t in range(PACK)]
-        for b in range(2):
-            for e in range(2):
-                product(y_acc[b][:, e, :], w1_mx, 2 * b + e, offs_mx)
-            for e in range(2):
-                nc.vector.tensor_copy(out=y_rows[2 * b + e][:], in_=y_acc[b][:, e, :])
-        denom_23 = keep.tile([P, 2, S], F32, name="denom_23", tag="w1_codes", align_bytes=64)
-        for t in range(2):
-            denominator(2 + t, denom_23[:, t, :])
-        y_fetched = keep.tile([P, 2, PACK, HALF], F32, name="y_fetched", tag="w1_codes", align_bytes=64)
-        for half in range(2):
+        y_rows = [keep.tile([P, S], F32, name=f"y_rows{t}", align_bytes=64) for t in range(PACK)]
+        for t in range(PACK):
+            product(y_acc[t // 2][:, t % 2, :], w1_mx, t, (offs_mx[0][:], offs_mx[1][:]))
+        for t in range(PACK):
+            nc.vector.tensor_copy(out=y_rows[t][:], in_=y_acc[t // 2][:, t % 2, :])
+        for t, slot in ((2, "w1_codes"), (3, "w1_scales")):
+            denom = keep.tile([P, S], F32, name=f"denom_{t}", tag=slot, align_bytes=64)
+            denominator(t, denom[:])
+        y_fetched = []
+        for (first, width), slot in zip(PIECES, ("y_fetched0", "w1_codes")):
+            fetched = keep.tile([P, PACK, width], F32, name=f"y_fetched{first}", tag=slot, align_bytes=64)
+            y_fetched.append(fetched)
             for t in range(PACK):
                 nc.scalar.activation(
-                    y_fetched[:, half, t, :], y_rows[t][:].indirect(half_list(n1_sb, half)), ACT.Copy
+                    fetched[:, t, :],
+                    y_rows[t][:].indirect(n1_sb[:, first // 16 : (first + width) // 16]),
+                    ACT.Copy,
                 )
+
         w3_mx = mx_tiles("w3", N)
-        w3_rounded = [keep.tile([P, PACK * P], BF16, name=f"w3_rounded{t}", align_bytes=64) for t in range(PACK)]
+        w3_rounded = {}
 
         def round_w3(t):
-            nc.vector.tensor_copy(
+            w3_rounded[t] = keep.tile([P, PACK * P], BF16, name=f"w3_rounded{t}", tag=f"y_rows{t}", align_bytes=64)
+            nc.scalar.copy(
                 out=w3_rounded[t][:].rearrange("p (c i j) -> p c j i", i=4, j=PACK),
                 in_=w3_raw[:, :, P * t : P * (t + 1)].rearrange("p j (c i) -> p c j i", i=4),
             )
@@ -186,70 +192,89 @@ def tile_picked_twlnormbtwice_none_p_kernel(tc, x_words, x_scales, w1, w2, gn, w
             cols = slice(P * t, P * (t + 1))
             nc.vector.quantize_mx(out=w3_mx[0][:, cols].bitcast(FP8X4), scales=w3_mx[1][:, cols], in_=w3_rounded[t][:])
 
-        round_w3(0)
+        for t in range(PACK):
+            round_w3(t)
         gain_over_denominator(0)
         gain_over_denominator(1)
-        quantise_w3(0)
-        gain_over_denominator(2)
-        round_w3(1)
-        gain_over_denominator(3)
-        quantise_w3(1)
-
-        z_rounded = keep.tile([P, PACK * S], BF16, name="z_rounded", align_bytes=64)
-        z_mx = mx_tiles("z", S)
-        for half in range(2):
-            cols = slice(half * HALF, (half + 1) * HALF)
-            diff = keep.tile([P, PACK, HALF], F32, name=f"diff{half}")
-            for b in range(2):
-                nc.vector.tensor_tensor(
-                    out=diff[:, 2 * b : 2 * b + 2, :], in0=y_acc[b][:, :, cols],
-                    in1=y_fetched[:, half, 2 * b : 2 * b + 2, :], op=ALU.subtract,
-                )
-                if half == 1 and b == 0:
-                    quantise(*z_mx, z_rounded, 0, HALF)
-            nc.vector.tensor_tensor(
-                out=z_rounded[:, half * PACK * HALF : (half + 1) * PACK * HALF].rearrange(
-                    "p (c i t) -> p c t i", i=4, t=PACK
-                ),
-                in0=diff[:].rearrange("p t (c i) -> p c t i", i=4),
-                in1=factor[:, :, cols].rearrange("p t (c i) -> p c t i", i=4),
-                op=ALU.mult,
-            )
-        round_w3(2)
-        quantise(*z_mx, z_rounded, HALF, HALF)
-        quantise_w3(2)
 
         h_acc = [psum.tile([P, S], F32, name=f"h_acc{t}", tag=f"bank{t}") for t in range(PACK)]
         h_fetched = [keep.tile([P, S], F32, name=f"h_fetched{t}") for t in range(PACK)]
         st_fetched = [keep.tile([P, S], F32, name=f"st_fetched{t}") for t in range(PACK)]
+        z_rounded = keep.tile([P, PACK * S], BF16, name="z_rounded", align_bytes=64)
+        z_mx = mx_tiles("z", S)
+
+        def h_columns(t, cols):
+            product(h_acc[t][:, cols], w3_mx, t, (z_mx[0][:, cols], z_mx[1][:, cols]))
+            nc.vector.tensor_copy(out=h_rows[t][:, cols], in_=h_acc[t][:, cols])
+
+        for n, (first, width) in enumerate(PIECES):
+            cols = slice(first, first + width)
+            diff = keep.tile([P, PACK, width], F32, name=f"diff{first}")
+            for b in range(2):
+                nc.vector.tensor_tensor(
+                    out=diff[:, 2 * b : 2 * b + 2, :], in0=y_acc[b][:, :, cols],
+                    in1=y_fetched[n][:, 2 * b : 2 * b + 2, :], op=ALU.subtract,
+                )
+                if b == 0 and n > 0:
+                    quantise(*z_mx, z_rounded, *PIECES[n - 1])
+            if n == 0:
+                gain_over_denominator(2)
+                gain_over_denominator(3)
+            if n == 1:
+                quantise_w3(0)
+            nc.vector.tensor_tensor(
+                out=z_rounded[:, PACK * first : PACK * (first + width)].rearrange("p (c i t) -> p c t i", i=4, t=PACK),
+                in0=diff[:].rearrange("p t (c i) -> p c t i", i=4),
+                in1=factor[:, :, cols].rearrange("p t (c i) -> p c t i", i=4),
+                op=ALU.mult,
+            )
+        h_columns(0, slice(0, HALF))
+        quantise(*z_mx, z_rounded, *PIECES[-1])
+        quantise_w3(1)
+        quantise_w3(2)
+
+        def fetch_h(t):
+            nc.scalar.activation(h_fetched[t][:], h_rows[t][:].indirect(n3_sb[:]), ACT.Copy)
 
         def make_h(t):
-            product(h_acc[t][:], w3_mx, t, z_mx)
-            nc.vector.tensor_copy(out=h_rows[t][:, :S], in_=h_acc[t][:])
-            nc.scalar.activation(h_fetched[t][:], h_rows[t][:].indirect(n3_sb[:]), ACT.Copy)
+            h_columns(t, slice(0, S))
+            fetch_h(t)
 
         def make_st(t):
             nc.vector.tensor_tensor(out=st_rows[t][:, :S], in0=h_acc[t][:], in1=h_fetched[t][:], op=ALU.subtract)
-            nc.scalar.activation(st_fetched[t][:], st_rows[t][:].indirect(n3_sb[:]), ACT.Copy)
 
-        def make_out(t):
-            result = keep.tile([P, S], F32, name=f"result{t}")
-            nc.vector.scalar_tensor_tensor(
-                out=result[:], in0=st_fetched[t][:], scalar=-0.5, in1=st_rows[t][:, :S], op0=ALU.mult, op1=ALU.add
+        def fetch_st(t, first, width):
+            nc.scalar.activation(
+                st_fetched[t][:, first : first + width],
+                st_rows[t][:].indirect(n3_sb[:, first // 16 : (first + width) // 16]),
+                ACT.Copy,
             )
-            nc.sync.dma_start(out=out[P * t : P * (t + 1), :], in_=result[:])
 
-        make_h(0)
+        def make_out(t, first, width):
+            cols = slice(first, first + width)
+            result = keep.tile([P, width], F32, name=f"result{t}_{first}")
+            nc.vector.scalar_tensor_tensor(
+                out=result[:], in0=st_fetched[t][:, cols], scalar=-0.5, in1=st_rows[t][:, cols], op0=ALU.mult, op1=ALU.add
+            )
+            nc.sync.dma_start(out=out[P * t : P * (t + 1), cols], in_=result[:])
+
+        h_columns(0, slice(HALF, S))
+        fetch_h(0)
         make_h(1)
-        round_w3(3)
-        make_st(0)
         quantise_w3(3)
         make_h(2)
+        make_st(0)
+        fetch_st(0, 0, S)
         make_st(1)
+        fetch_st(1, 0, S)
         make_h(3)
-        make_out(0)
+        make_out(0, 0, S)
         make_st(2)
-        make_out(1)
+        fetch_st(2, 0, S)
+        make_out(1, 0, S)
         make_st(3)
-        make_out(2)
-        make_out(3)
+        fetch_st(3, 0, HALF)
+        fetch_st(3, HALF, HALF)
+        make_out(2, 0, S)
+        make_out(3, 0, HALF)
+        make_out(3, HALF, HALF)

@@ -42,13 +42,15 @@ def tile_picked_twlnormbtwice_none_p_kernel(tc, x_words, x_scales, w1, w2, gn, w
         w2_raw = keep.tile([P, PACK, H], F32, name="w2_raw")
         w3_raw = keep.tile([P, PACK, N], F32, name="w3_raw")
         gain = keep.tile([P, PACK], F32, name="gain")
+        d_abs = [keep.tile([P, 2 * S], F32, name=f"d_abs{t}") for t in range(PACK)]
         h_rows = [keep.tile([P, S + SPARE], F32, name=f"h_rows{t}") for t in range(PACK)]
         st_rows = [keep.tile([P, S + SPARE], F32, name=f"st_rows{t}") for t in range(PACK)]
 
         nc.vector.memset(scale_table[:].bitcast(I32), 0)
-        for list_sb, list_in in ((two_sb, two), (offs_sb, offs), (n2_sb, n2)):
-            nc.sync.dma_start(list_sb[:], list_in)
+        nc.sync.dma_start(two_sb[:], two)
         nc.sync.dma_start(out=w2_raw[:], in_=w2.rearrange("(p j) c -> p j c", j=PACK))
+        nc.sync.dma_start(offs_sb[:], offs)
+        nc.sync.dma_start(n2_sb[:], n2)
         for r in range(4):
             nc.sync.dma_start(
                 out=scale_table[r:P:32, :].bitcast(I32),
@@ -66,7 +68,7 @@ def tile_picked_twlnormbtwice_none_p_kernel(tc, x_words, x_scales, w1, w2, gn, w
         nc.sync.dma_start(out=w3_raw[:], in_=w3.rearrange("(p j) c -> p j c", j=PACK))
         nc.sync.dma_start(n3_sb[:], n3)
         nc.sync.dma_start(out=gain[:], in_=gn.rearrange("(p t) o -> p (t o)", t=PACK))
-        for rows in h_rows + st_rows:
+        for rows in h_rows + st_rows + d_abs:
             nc.vector.memset(rows[:, S:], 0.0)
         warm = keep.tile([P, SPARE], F32, name="warm")
         nc.scalar.activation(warm[:], h_rows[0][:, S:], ACT.Abs_reciprocal_sqrt, bias=1.0)
@@ -103,8 +105,8 @@ def tile_picked_twlnormbtwice_none_p_kernel(tc, x_words, x_scales, w1, w2, gn, w
 
         w2_rounded = keep.tile([P, PACK * H], BF16, name="w2_rounded", align_bytes=64)
         dst, src = dealt_views(w2_rounded, w2_raw)
-        nc.vector.tensor_copy(out=dst[:, :42], in_=src[:, :42])
-        nc.scalar.copy(out=dst[:, 42:], in_=src[:, 42:])
+        nc.vector.tensor_copy(out=dst[:, :52], in_=src[:, :52])
+        nc.scalar.copy(out=dst[:, 52:], in_=src[:, 52:])
         w2_mx = mx_tiles("w2", H)
         two_mx = mx_tiles("x_two", S)
         nc.vector.tensor_copy(two_mx[1][:], scale_table[:].indirect(two_sb[:]))
@@ -114,27 +116,18 @@ def tile_picked_twlnormbtwice_none_p_kernel(tc, x_words, x_scales, w1, w2, gn, w
         nc.vector.tensor_copy(offs_mx[1][:], scale_table[:].indirect(offs_sb[:]))
         nc.vector.tensor_copy(offs_mx[0][:], x_table[:].indirect(offs_sb[:]))
 
-        def half_list(list_sb, half):
-            return list_sb[:, half * LIST_COLS // 2 : (half + 1) * LIST_COLS // 2]
-
         d_fetched = keep.tile([P, PACK, S], F32, name="d_fetched")
         root = keep.tile([P, PACK, S], F32, name="root")
-        factor = keep.tile([P, PACK, S], F32, name="factor")
-        d_abs = [keep.tile([P, S], F32, name=f"d_abs{t}") for t in range(PACK)]
+        factor = keep.tile([P, PACK, S], F32, name="factor", align_bytes=64)
         for t in range(PACK):
             d_acc = psum.tile([P, S], F32, name=f"d_acc{t}", tag=f"bank{t}")
             product(d_acc[:], w2_mx, t, (two_mx[0][:], two_mx[1][:]))
-            nc.scalar.activation(d_abs[t][:], d_acc[:], ACT.Abs)
-            for half in range(2):
-                nc.scalar.activation(
-                    d_fetched[:, t, half * HALF : (half + 1) * HALF],
-                    d_abs[t][:].indirect(half_list(n2_sb, half)),
-                    ACT.Copy,
-                )
+            nc.scalar.activation(d_abs[t][:, :S], d_acc[:], ACT.Abs)
+            nc.scalar.activation(d_fetched[:, t, :], d_abs[t][:].indirect(n2_sb[:]), ACT.Copy)
 
         def denominator(t, denom):
             nc.vector.scalar_tensor_tensor(
-                out=denom, in0=d_abs[t][:], scalar=0.5, in1=d_fetched[:, t, :], op0=ALU.add, op1=ALU.add
+                out=denom, in0=d_abs[t][:, :S], scalar=0.5, in1=d_fetched[:, t, :], op0=ALU.add, op1=ALU.add
             )
             nc.scalar.activation(root[:, t, :], denom, ACT.Abs_reciprocal_sqrt)
 
@@ -181,9 +174,9 @@ def tile_picked_twlnormbtwice_none_p_kernel(tc, x_words, x_scales, w1, w2, gn, w
         w3_mx = mx_tiles("w3", N)
         w3_rounded = {}
 
-        def round_w3(t):
-            w3_rounded[t] = keep.tile([P, PACK * P], BF16, name=f"w3_rounded{t}", tag=f"y_rows{t}", align_bytes=64)
-            nc.scalar.copy(
+        def round_w3(t, slot, copy):
+            w3_rounded[t] = keep.tile([P, PACK * P], BF16, name=f"w3_rounded{t}", tag=slot, align_bytes=64)
+            copy(
                 out=w3_rounded[t][:].rearrange("p (c i j) -> p c j i", i=4, j=PACK),
                 in_=w3_raw[:, :, P * t : P * (t + 1)].rearrange("p j (c i) -> p c j i", i=4),
             )
@@ -192,10 +185,11 @@ def tile_picked_twlnormbtwice_none_p_kernel(tc, x_words, x_scales, w1, w2, gn, w
             cols = slice(P * t, P * (t + 1))
             nc.vector.quantize_mx(out=w3_mx[0][:, cols].bitcast(FP8X4), scales=w3_mx[1][:, cols], in_=w3_rounded[t][:])
 
-        for t in range(PACK):
-            round_w3(t)
+        for t in (1, 3):
+            round_w3(t, f"y_rows{t}", nc.scalar.copy)
         gain_over_denominator(0)
         gain_over_denominator(1)
+        round_w3(0, "w1_rounded", nc.vector.tensor_copy)
 
         h_acc = [psum.tile([P, S], F32, name=f"h_acc{t}", tag=f"bank{t}") for t in range(PACK)]
         h_fetched = [keep.tile([P, S], F32, name=f"h_fetched{t}") for t in range(PACK)]
@@ -209,7 +203,7 @@ def tile_picked_twlnormbtwice_none_p_kernel(tc, x_words, x_scales, w1, w2, gn, w
 
         for n, (first, width) in enumerate(PIECES):
             cols = slice(first, first + width)
-            diff = keep.tile([P, PACK, width], F32, name=f"diff{first}")
+            diff = keep.tile([P, PACK, width], F32, name=f"diff{first}", align_bytes=64)
             for b in range(2):
                 nc.vector.tensor_tensor(
                     out=diff[:, 2 * b : 2 * b + 2, :], in0=y_acc[b][:, :, cols],
@@ -220,8 +214,9 @@ def tile_picked_twlnormbtwice_none_p_kernel(tc, x_words, x_scales, w1, w2, gn, w
             if n == 0:
                 gain_over_denominator(2)
                 gain_over_denominator(3)
-            if n == 1:
                 quantise_w3(0)
+            if n == 1:
+                round_w3(2, "diff0", nc.vector.tensor_copy)
             nc.vector.tensor_tensor(
                 out=z_rounded[:, PACK * first : PACK * (first + width)].rearrange("p (c i t) -> p c t i", i=4, t=PACK),
                 in0=diff[:].rearrange("p t (c i) -> p c t i", i=4),

from contextlib import ExitStack

import concourse.mybir as mybir

K, T, S, H, N = 512, 2048, 256, 512, 512
FLOPS = 2 * K * H * S * 2 + 2 * H * N * S

F32 = mybir.dt.float32
BF16 = mybir.dt.bfloat16
I32 = mybir.dt.int32
U32 = mybir.dt.uint32
U16 = mybir.dt.uint16
U8 = mybir.dt.uint8
FP8X4 = mybir.dt.float8_e4m3fn_x4
ALU = mybir.AluOpType
ACT = mybir.ActivationFunctionType

P = 128
PACK = 4
HALF = S // 2
LIST_COLS = S // 16
SPARE = 8
PIECES = ((0, 128), (128, 128))


def tile_picked_twlnormbtwice_none_p_kernel(tc, x_words, x_scales, w1, w2, gn, w3, offs, two, n1, n2, n3, out):
    nc = tc.nc
    with ExitStack() as ctx:
        lists = ctx.enter_context(tc.tile_pool(name="lists", bufs=1))
        keep = ctx.enter_context(tc.tile_pool(name="keep", bufs=1))
        psum = ctx.enter_context(tc.psum_pool(name="psum", bufs=1))

        offs_sb = lists.tile([P, LIST_COLS], U16, name="offs_sb")
        two_sb = lists.tile([P, LIST_COLS], U16, name="two_sb")
        n1_sb = lists.tile([P, LIST_COLS], U16, name="n1_sb")
        n2_sb = lists.tile([P, LIST_COLS], U16, name="n2_sb")
        n3_sb = lists.tile([P, LIST_COLS], U16, name="n3_sb")

        x_table = keep.tile([P, T], U32, name="x_table")
        scale_table = keep.tile([P, T], U8, name="scale_table")
        w1_raw = [keep.tile([P, PACK, H // 2], F32, name=f"w1_raw{half}") for half in range(2)]
        w2_raw = keep.tile([P, PACK, H], F32, name="w2_raw")
        w3_raw = keep.tile([P, PACK, N], F32, name="w3_raw")
        gain = keep.tile([P, PACK], F32, name="gain")
        d_abs = [keep.tile([P, 2 * S], F32, name=f"d_abs{t}") for t in range(PACK)]
        h_rows = [keep.tile([P, S + SPARE], F32, name=f"h_rows{t}") for t in range(PACK)]
        st_rows = [keep.tile([P, S + SPARE], F32, name=f"st_rows{t}") for t in range(PACK)]

        nc.vector.memset(scale_table[:].bitcast(I32), 0)
        nc.sync.dma_start(two_sb[:], two)
        nc.sync.dma_start(out=w2_raw[:], in_=w2.rearrange("(p j) c -> p j c", j=PACK))
        nc.sync.dma_start(offs_sb[:], offs)
        nc.sync.dma_start(n2_sb[:], n2)
        for r in range(4):
            nc.sync.dma_start(
                out=scale_table[r:P:32, :].bitcast(I32),
                in_=x_scales[0, r:16:4, :].bitcast(I32),
            )
        nc.sync.dma_start(
            out=x_table[:].bitcast(I32), in_=x_words[0].rearrange("p n t -> p (n t)").bitcast(I32)
        )
        for half in range(2):
            nc.sync.dma_start(
                out=w1_raw[half][:],
                in_=w1[:, half * H // 2 : (half + 1) * H // 2].rearrange("(p j) c -> p j c", j=PACK),
            )
        nc.sync.dma_start(n1_sb[:], n1)
        nc.sync.dma_start(out=w3_raw[:], in_=w3.rearrange("(p j) c -> p j c", j=PACK))
        nc.sync.dma_start(n3_sb[:], n3)
        nc.sync.dma_start(out=gain[:], in_=gn.rearrange("(p t) o -> p (t o)", t=PACK))
        for rows in h_rows + st_rows + d_abs:
            nc.vector.memset(rows[:, S:], 0.0)
        warm = keep.tile([P, SPARE], F32, name="warm")
        nc.scalar.activation(warm[:], h_rows[0][:, S:], ACT.Abs_reciprocal_sqrt, bias=1.0)

        def mx_tiles(name, width):
            codes = keep.tile([P, width], U32, name=name + "_codes", align_bytes=64)
            scales = keep.tile([P, width], U8, name=name + "_scales", align_bytes=64)
            return codes, scales

        def quantise(codes, scales, rounded, first, width):
            nc.vector.quantize_mx(
                out=codes[:, first : first + width].bitcast(FP8X4),
                scales=scales[:, first : first + width],
                in_=rounded[:, PACK * first : PACK * (first + width)],
            )

        def product(acc, w_mx, t, moving_mx):
            cols = slice(P * t, P * (t + 1))
            nc.tensor.matmul_mx(
                out=acc,
                lhsT=w_mx[0][:, cols].bitcast(FP8X4),
                lhsT_scale=w_mx[1][:, cols],
                rhs=moving_mx[0].bitcast(FP8X4),
                rhs_scale=moving_mx[1],
                start=True,
                stop=True,
            )

        def dealt_views(rounded, raw):
            return (
                rounded[:].rearrange("p (t m i j) -> p m j i t", t=PACK, i=2, j=PACK),
                raw[:].rearrange("p j (m i t) -> p m j i t", i=2, t=PACK),
            )

        w2_rounded = keep.tile([P, PACK * H], BF16, name="w2_rounded", align_bytes=64)
        dst, src = dealt_views(w2_rounded, w2_raw)
        nc.vector.tensor_copy(out=dst[:, :52], in_=src[:, :52])
        nc.scalar.copy(out=dst[:, 52:], in_=src[:, 52:])
        w2_mx = mx_tiles("w2", H)
        two_mx = mx_tiles("x_two", S)
        nc.vector.tensor_copy(two_mx[1][:], scale_table[:].indirect(two_sb[:]))
        quantise(*w2_mx, w2_rounded, 0, H)
        nc.vector.tensor_copy(two_mx[0][:], x_table[:].indirect(two_sb[:]))
        offs_mx = mx_tiles("x_offs", S)
        nc.vector.tensor_copy(offs_mx[1][:], scale_table[:].indirect(offs_sb[:]))
        nc.vector.tensor_copy(offs_mx[0][:], x_table[:].indirect(offs_sb[:]))

        d_fetched = keep.tile([P, PACK, S], F32, name="d_fetched")
        root = keep.tile([P, PACK, S], F32, name="root")
        factor = keep.tile([P, PACK, S], F32, name="factor", align_bytes=64)
        for t in range(PACK):
            d_acc = psum.tile([P, S], F32, name=f"d_acc{t}", tag=f"bank{t}")
            product(d_acc[:], w2_mx, t, (two_mx[0][:], two_mx[1][:]))
            nc.scalar.activation(d_abs[t][:, :S], d_acc[:], ACT.Abs)
            nc.scalar.activation(d_fetched[:, t, :], d_abs[t][:].indirect(n2_sb[:]), ACT.Copy)

        def denominator(t, denom):
            nc.vector.scalar_tensor_tensor(
                out=denom, in0=d_abs[t][:, :S], scalar=0.5, in1=d_fetched[:, t, :], op0=ALU.add, op1=ALU.add
            )
            nc.scalar.activation(root[:, t, :], denom, ACT.Abs_reciprocal_sqrt)

        def gain_over_denominator(t):
            nc.vector.scalar_tensor_tensor(
                out=factor[:, t, :], in0=root[:, t, :], scalar=gain[:, t : t + 1], in1=root[:, t, :],
                op0=ALU.mult, op1=ALU.mult,
            )

        w1_rounded = keep.tile([P, PACK * H], BF16, name="w1_rounded", align_bytes=64)
        dst = w1_rounded[:].rearrange("p (t m i j) -> p m j i t", t=PACK, i=2, j=PACK)
        for half in range(2):
            nc.vector.tensor_copy(
                out=dst[:, half * P // 4 : (half + 1) * P // 4],
                in_=w1_raw[half][:].rearrange("p j (m i t) -> p m j i t", i=2, t=PACK),
            )
        w1_mx = mx_tiles("w1", H)
        for b in range(2):
            quantise(*w1_mx, w1_rounded, 2 * P * b, 2 * P)
        denom_01 = keep.tile([P, 2, S], F32, name="denom_01", tag="w1_raw1")
        for t in range(2):
            denominator(t, denom_01[:, t, :])

        y_acc = [psum.tile([P, 2, S], F32, name=f"y_acc{b}", tag=f"y_bank{b}") for b in range(2)]
        y_rows = [keep.tile([P, S], F32, name=f"y_rows{t}", align_bytes=64) for t in range(PACK)]
        for t in range(PACK):
            product(y_acc[t // 2][:, t % 2, :], w1_mx, t, (offs_mx[0][:], offs_mx[1][:]))
        for t in range(PACK):
            nc.vector.tensor_copy(out=y_rows[t][:], in_=y_acc[t // 2][:, t % 2, :])
        for t, slot in ((2, "w1_codes"), (3, "w1_scales")):
            denom = keep.tile([P, S], F32, name=f"denom_{t}", tag=slot, align_bytes=64)
            denominator(t, denom[:])
        y_fetched = []
        for (first, width), slot in zip(PIECES, ("y_fetched0", "w1_codes")):
            fetched = keep.tile([P, PACK, width], F32, name=f"y_fetched{first}", tag=slot, align_bytes=64)
            y_fetched.append(fetched)
            for t in range(PACK):
                nc.scalar.activation(
                    fetched[:, t, :],
                    y_rows[t][:].indirect(n1_sb[:, first // 16 : (first + width) // 16]),
                    ACT.Copy,
                )

        w3_mx = mx_tiles("w3", N)
        w3_rounded = {}

        def round_w3(t, slot, copy):
            w3_rounded[t] = keep.tile([P, PACK * P], BF16, name=f"w3_rounded{t}", tag=slot, align_bytes=64)
            copy(
                out=w3_rounded[t][:].rearrange("p (c i j) -> p c j i", i=4, j=PACK),
                in_=w3_raw[:, :, P * t : P * (t + 1)].rearrange("p j (c i) -> p c j i", i=4),
            )

        def quantise_w3(t):
            cols = slice(P * t, P * (t + 1))
            nc.vector.quantize_mx(out=w3_mx[0][:, cols].bitcast(FP8X4), scales=w3_mx[1][:, cols], in_=w3_rounded[t][:])

        for t in (1, 3):
            round_w3(t, f"y_rows{t}", nc.scalar.copy)
        gain_over_denominator(0)
        gain_over_denominator(1)
        round_w3(0, "w1_rounded", nc.vector.tensor_copy)

        h_acc = [psum.tile([P, S], F32, name=f"h_acc{t}", tag=f"bank{t}") for t in range(PACK)]
        h_fetched = [keep.tile([P, S], F32, name=f"h_fetched{t}") for t in range(PACK)]
        st_fetched = [keep.tile([P, S], F32, name=f"st_fetched{t}") for t in range(PACK)]
        z_rounded = keep.tile([P, PACK * S], BF16, name="z_rounded", align_bytes=64)
        z_mx = mx_tiles("z", S)

        def h_columns(t, cols):
            product(h_acc[t][:, cols], w3_mx, t, (z_mx[0][:, cols], z_mx[1][:, cols]))
            nc.vector.tensor_copy(out=h_rows[t][:, cols], in_=h_acc[t][:, cols])

        for n, (first, width) in enumerate(PIECES):
            cols = slice(first, first + width)
            diff = keep.tile([P, PACK, width], F32, name=f"diff{first}", align_bytes=64)
            for b in range(2):
                nc.vector.tensor_tensor(
                    out=diff[:, 2 * b : 2 * b + 2, :], in0=y_acc[b][:, :, cols],
                    in1=y_fetched[n][:, 2 * b : 2 * b + 2, :], op=ALU.subtract,
                )
                if b == 0 and n > 0:
                    quantise(*z_mx, z_rounded, *PIECES[n - 1])
            if n == 0:
                gain_over_denominator(2)
                gain_over_denominator(3)
                quantise_w3(0)
            if n == 1:
                round_w3(2, "diff0", nc.vector.tensor_copy)
            nc.vector.tensor_tensor(
                out=z_rounded[:, PACK * first : PACK * (first + width)].rearrange("p (c i t) -> p c t i", i=4, t=PACK),
                in0=diff[:].rearrange("p t (c i) -> p c t i", i=4),
                in1=factor[:, :, cols].rearrange("p t (c i) -> p c t i", i=4),
                op=ALU.mult,
            )
        h_columns(0, slice(0, HALF))
        quantise(*z_mx, z_rounded, *PIECES[-1])
        quantise_w3(1)
        quantise_w3(2)

        def fetch_h(t):
            nc.scalar.activation(h_fetched[t][:], h_rows[t][:].indirect(n3_sb[:]), ACT.Copy)

        def make_h(t):
            h_columns(t, slice(0, S))
            fetch_h(t)

        def make_st(t):
            nc.vector.tensor_tensor(out=st_rows[t][:, :S], in0=h_acc[t][:], in1=h_fetched[t][:], op=ALU.subtract)

        def fetch_st(t, first, width):
            nc.scalar.activation(
                st_fetched[t][:, first : first + width],
                st_rows[t][:].indirect(n3_sb[:, first // 16 : (first + width) // 16]),
                ACT.Copy,
            )

        def make_out(t, first, width):
            cols = slice(first, first + width)
            result = keep.tile([P, width], F32, name=f"result{t}_{first}")
            nc.vector.scalar_tensor_tensor(
                out=result[:], in0=st_fetched[t][:, cols], scalar=-0.5, in1=st_rows[t][:, cols], op0=ALU.mult, op1=ALU.add
            )
            nc.sync.dma_start(out=out[P * t : P * (t + 1), cols], in_=result[:])

        h_columns(0, slice(HALF, S))
        fetch_h(0)
        make_h(1)
        quantise_w3(3)
        make_h(2)
        make_st(0)
        fetch_st(0, 0, S)
        make_st(1)
        fetch_st(1, 0, S)
        make_h(3)
        make_out(0, 0, S)
        make_st(2)
        fetch_st(2, 0, S)
        make_out(1, 0, S)
        make_st(3)
        fetch_st(3, 0, HALF)
        fetch_st(3, HALF, HALF)
        make_out(2, 0, S)
        make_out(3, 0, HALF)
        make_out(3, HALF, HALF)
